import numpy as np, ml_dtypes
CORES = [23,119,17,113]
N = 4
BF = ml_dtypes.bfloat16
def gentries(a):
    return np.ascontiguousarray(a.reshape(8, 16, -1).transpose(0, 2, 1)).reshape(8, -1)
def gtable(e):
    e = np.asarray(e); return np.ascontiguousarray(e.reshape(8, -1, 16).transpose(0, 2, 1)).reshape(128, -1).astype(np.int32)
V, R, K, S, RO = 4096, 4096, 1024, 4, 3
def take(a, j):
    return np.take_along_axis(a, j, 2)
def parts(rng, x):
    rec = rng.integers(0, R, (N, 8, V)); pri = take(np.sum(x, axis=2), rec); m = V - 1; q = np.arange(m)
    o = 1 + np.argsort(-pri[..., 1:], axis=2, kind="stable"); ch = []
    for side in range(2):
        u = rng.random((N, 8, m)); p = np.minimum(q + 1 + ((m - 1 - q) * u * u * u).astype(np.int64), m - 1)
        k = np.where((rng.random((N, 8, m)) < 0.1) | (q == m - 1), 0, take(o, p))
        a = rng.integers(0, V, (N, 8, V)); np.put_along_axis(a, o, k, 2); ch.append(a)
    u = rng.random((N, 8, K)); rt = np.where(rng.random((N, 8, K)) < 0.03, 0, take(o, (m * u * u).astype(np.int64)))
    return rec, ch[0], ch[1], rt, rng.integers(0, 256, (N, 8, 16))
def people(rng):
    big = rng.random((N, 8, 16, K)) < 0.35
    return np.where(rng.random((N, 8, 1, K)) < 0.5, rng.integers(0, 16, big.shape), np.where(big, rng.integers(12, 16, big.shape), rng.integers(0, 7, big.shape)))
def pack(x, y, rec, lc, rc, rt, w):
    return {"x": np.ascontiguousarray(x).reshape(N, 128, R).astype(BF), "nw": np.ascontiguousarray(y).reshape(N, 128, K).astype(BF),
            "rec": rec.astype(np.int32), "lc": lc.astype(np.int32), "rc": rc.astype(np.int32), "rt": np.stack([gtable(a) for a in rt]),
            "wt": np.ascontiguousarray(w).reshape(N, 128, 1).astype(np.int32)}
def setup_inputs(rng):
    x = rng.integers(0, 16, (N, 8, 16, R))
    return pack(x, people(rng), *parts(rng, x))
def setup_inputs_ties(rng):
    c = [[8] * 8 + [7, 7, 6, 6, 6, 6, 5, 5], [8] * 8 + [7, 7, 6, 6, 6, 5, 5, 5], [9] + [8] * 7 + [7, 7, 6, 6, 6, 6, 5, 5],
         [8] * 9 + [6, 6, 6, 6, 6, 5, 5], [8] * 9 + [6, 6, 6, 6, 5, 5, 5], [9] + [8] * 8 + [6, 6, 6, 6, 6, 5, 5]]
    a = np.array(c)[rng.integers(0, 6, (N, 8, R))]
    x = np.take_along_axis(a, np.argsort(rng.random(a.shape), axis=3), 3).transpose(0, 1, 3, 2)
    u = rng.random((N, 8, 1, R)); x = np.where(u < 0.06, 0, np.where(u > 0.94, np.where(rng.random(x.shape) < 0.2, 14, 15), x))
    rec, lc, rc, rt, w = parts(rng, x)
    lc = rng.integers(0, V, lc.shape); rc = rng.integers(0, V, rc.shape)
    u = rng.random((N, 8, 1, K)); y = np.where(u < 0.6, 7, people(rng))
    return pack(x, np.where(u > 0.9, np.where(rng.random(y.shape) < 0.15, 14, 15), y), rec, lc, rc, rt, w)
def setup_inputs_ends(rng):
    x = rng.integers(0, 16, (N, 8, 16, R)); rec, lc, rc, rt, w = parts(rng, x)
    lc = np.where(rng.random(lc.shape) < 0.4, 0, lc); rc = np.where(rng.random(rc.shape) < 0.4, 0, rc)
    e = np.array([0, 1, V - 1])
    lc[:, 1] = rng.choice(e, (N, V)); rc[:, 1] = rng.choice(e, (N, V)); rt[:, 1] = rng.choice(e, (N, K))
    rec[:, 2] = rng.choice(np.array([0, R - 1]), (N, V)); rt[:, 3] = rng.choice(e, (N, K))
    rec[:, 4:, 1] = R - 1; rec[:, 4:, V - 1] = 0; rt[:, 5, 0] = V - 1; rt[:, 5, K - 1] = 1
    for q in range(N): rt[q, (q + int(rng.integers(0, 2))) % 8] = 0
    return pack(x, people(rng), rec, lc, rc, rt, w)
def setup_inputs_long(rng):
    x = rng.integers(0, 16, (N, 8, 16, R)); y = people(rng); half = R // 2
    x[:, 0] = rng.integers(1, 16, (N, 16, R)); y[:, 0] = 0
    y[:, 1] = 15; x[:, 1, :, ::16] = 15
    x[:, 2] = rng.integers(9, 16, (N, 16, R)); y[:, 2, :9] = 15; y[:, 2, 9:] = 0
    x[:, 3, 7:] = rng.integers(1, 4, (N, 9, R)); y[:, 3, 7:] = 0; y[:, 3, :7] = 15
    for g in range(4, 8):
        x[:, g, :, :half] = rng.integers(9, 16, (N, 16, half)); x[:, g, :, half:] = rng.integers(0, 7, (N, 16, R - half))
        y[:, g] = np.where(rng.random((N, 1, K)) < 0.5, rng.integers(7, 9, (N, 16, K)), np.where(np.arange(16)[:, None] < 9, 15, 0))
    rec, lc, rc, rt, w = parts(rng, x); out = []
    for a in (lc, rc, rt): out.append(np.where(a == 0, rng.integers(1, V, a.shape), a))
    for g in range(4, 8):
        h = min(g - 3, S - 1); m = V // (h + 1); lev = np.arange(V) % (h + 1)
        for k in range(2): out[k][:, g] = np.where(lev < h, (h + 1) * rng.integers(0, m, (N, V)) + lev + 1, out[k][:, g])
        out[2][:, g] = (h + 1) * rng.integers(1, m, (N, K))
        rec[:, g] = rng.integers(0, half, (N, V)) + np.where(lev == h, half, 0)
    return pack(x, y, rec, out[0], out[1], out[2], w)
def setup_inputs_alike(rng):
    x = rng.integers(0, 16, (N, 8, 16, R)); rec, lc, rc, rt, w = parts(rng, x); y = people(rng); v = np.arange(V)
    rt[:, 0] = rng.integers(1, V, (N, 1)); rt[:, 2] = rng.choice(np.array([1, V - 1, 5]), (N, K))
    rec[:, 1] = rng.integers(0, R, (N, 1)); rec[:, 3] = rng.choice(np.array([0, R - 1, 17]), (N, V))
    lc[:, 4] = np.where(rng.random((N, V)) < 0.5, v, lc[:, 4]); rc[:, 5] = np.where(rng.random((N, V)) < 0.5, v, rc[:, 5]); rc[:, 6] = lc[:, 6]
    y[:, 7] = y[:, 7, :, :1]; y[:, 2, :, ::2] = y[:, 2, :, :1]
    w[0] = 0; w[1] = 255; w[2:] = 0; w[2:, :, int(rng.integers(0, 16))] = rng.integers(1, 256, (N - 2, 8))
    q = K // 4; rt[0, 3, :q] = 0
    y[0, 3, :, :q] = np.where((rng.random((16, q)) < 0.25) & (np.arange(q) % 2 == 1), 14, 15)
    return pack(x, y, rec, lc, rc, rt, w)
def setup_inputs_spread(rng):
    x = (16 * rng.random((N, 8, 16, R)) ** np.exp2(rng.integers(-2, 3, (N, 8, 1, R)))).astype(np.int64)
    y = (16 * rng.random((N, 8, 16, K)) ** np.exp2(rng.integers(-2, 3, (N, 8, 1, K)))).astype(np.int64)
    rec, lc, rc, rt, w = parts(rng, np.minimum(x, 15))
    return pack(np.minimum(x, 15), np.minimum(y, 15), rec, lc, rc, rt, np.minimum((256 * rng.random((N, 8, 16)) ** 4).astype(np.int64), 255))
def check_inputs(d):
    bad = []
    for k in ("x", "nw"):
        a = np.asarray(d[k]).astype(np.float32)
        if not bool(np.all((a >= 0) & (a <= 15) & (a == np.floor(a)))): bad.append("whole numbers and range of " + k)
    for k, hi in (("rec", R - 1), ("lc", V - 1), ("rc", V - 1), ("rt", V - 1), ("wt", 255)):
        if np.min(d[k]) < 0 or np.max(d[k]) > hi: bad.append("range of " + k)
    return bad
def reference(x, nw, rec, lc, rc, rt, wt):
    nodes = V + RO * (S + 1) * K; lane = np.zeros((N, 8, K), np.int64) + np.arange(K)
    xs = np.zeros((N, 8, 16, R + RO * K), np.int64); xs[..., :R] = x.astype(np.float32).astype(np.int64).reshape(N, 8, 16, R)
    y = nw.astype(np.float32).astype(np.int64).reshape(N, 8, 16, K); w = wt.astype(np.int64).reshape(N, 8, 16, 1)
    of = np.zeros((N, 8, nodes), np.int64); of[..., :V] = rec
    pt = np.zeros((N, 8, 2 * nodes + 2 * K), np.int64); pt[..., 0:2 * V:2] = lc; pt[..., 1:2 * V:2] = rc
    def put(m, at, v):
        np.put_along_axis(pt, np.where(m, at, 2 * nodes + K + lane), v, 2)
    c = np.stack([gentries(a) for a in rt]).astype(np.int64)
    for t in range(RO):
        b = V + t * (S + 1) * K; new = b + S * K + lane
        xs[..., R + t * K:R + (t + 1) * K] = y; of[..., b + S * K:b + (S + 1) * K] = R + t * K + lane
        py = np.sum(y, axis=2); hung = lane < 0; went = lane < 0; last = lane * 0
        hole = 2 * nodes + lane; lh = lane * 0; rh = lane * 0; opened = lane * 0
        for s in range(S):
            live = c > 0; n = b + s * K + lane; rn = take(of, c); xc = np.take_along_axis(xs, rn[:, :, None, :], 3)
            hang = live & ~hung & (np.sum(xc, axis=2) < py)
            put(hang, hole, new); lh = np.where(hang, 2 * new, lh); rh = np.where(hang, 2 * new + 1, rh); hung = hung | hang
            high = np.sum(xc > y, axis=2) >= 9
            l = take(pt, 2 * c); r = take(pt, 2 * c + 1)
            of[..., b + s * K:b + (s + 1) * K] = np.where(live, rn, 0); put(live, 2 * n, l); put(live, 2 * n + 1, r)
            put(live, np.where(hung, np.where(high, rh, lh), hole), n)
            opened = np.where(live, np.where(high, 2 * n, 2 * n + 1), opened)
            hole = np.where(live & ~hung, opened, hole)
            lh = np.where(live & hung & ~high, opened, lh); rh = np.where(live & hung & high, opened, rh)
            last = np.where(live, rn, last); went = went | live
            c = np.where(live, np.where(high, l, r), 0)
        xc = np.take_along_axis(xs, take(of, c)[:, :, None, :], 3); high = np.sum(xc > y, axis=2) >= 9
        put(~hung, hole, new); put(~hung & (c > 0), np.where(high, 2 * new + 1, 2 * new), c)
        put(hung, lh, 0); put(hung, rh, 0); put(hung, opened, c)
        made = np.array(pt[..., 2 * nodes:2 * nodes + K])
        if t < RO - 1:
            xl = np.where(went[:, :, None, :], np.take_along_axis(xs, last[:, :, None, :], 3), 0)
            y = np.roll((y + xl + t) & 15, 1, axis=0)
            c = take(made, np.sum(w * y, axis=2) & (K - 1))
    return {"yl": pt[..., 2 * V:2 * nodes:2].astype(np.float32), "yr": pt[..., 2 * V + 1:2 * nodes:2].astype(np.float32), "yt": made.astype(np.float32)}

from concourse.mybir import AluOpType as ALU, ActivationFunctionType as ACT

V, K = 4096, 1024
NT = V + 15 * K
F, BF, I32 = "float32", "bfloat16", "int32"
SCRATCH = {n: ("sbuf", list(sh), d) for n, sh, d in [
    ("xs", (128, V), BF), ("ta", (128, NT), BF), ("tb", (128, NT - K), BF), ("rtab", (128, K), BF), ("ra", (128, K), BF),
    ("gt", (128, K), BF), ("gt5", (128, K), BF), ("a5", (128, K), BF), ("sg", (128, K), BF), ("sb", (128, 2 * K), BF),
    ("reci", (128, 8, 32), I32), ("recf", (128, 16, 16), F), ("recw", (128, 256), "uint16"),
    ("lri", (128, 512), I32), ("lrf", (128, 512), F), ("lr0", (128, 512), BF), ("lr1", (128, 512), BF),
    ("rti", (128, 64), I32), ("wti", (128, 4), I32), ("wtf", (128, 4), F), ("off", (128, 256), "uint16"), ("ui", (128, 128), I32),
    ("z", (128, 32, 16), F), ("zb", (128, 144, 4), BF), ("ones", (128, 128), F), ("idf", (128, 128), F), ("idb", (128, 128), BF),
    ("n8", (128, 128), BF), ("n1", (128, 128), BF), ("sel", (128, 8), F), ("tmp8", (128, 32), F), ("rows", (128, 56), F),
    ("rme", (128, 72), BF), ("rg", (128, 32), BF), ("ws", (128, 16), BF), ("rm", (128, 32), F), ("rmb", (128, 128), BF),
    ("pari", (128, 8), I32), ("par", (128, 4), F), ("nz", (128, 4), F), ("bias", (128, 8), F),
    ("gid", (128, 240, 8), F), ("glp", (128, 64, 8), F), ("hi", (128, 136, 8), F), ("pr", (128, 128, 8), F), ("nk", (128, 64, 8), F),
    ("py", (128, 8, 8), F), ("wk", (128, 128, 8), F), ("lx", (128, 16, 24), F), ("ly", (128, 32, 16), F),
    ("ox", (128, 512), F), ("oy", (128, 512), F), ("sx0", (128, 512), BF), ("sx1", (128, 512), BF), ("sy0", (128, 512), BF), ("sy1", (128, 512), BF)]}
SCRATCH.update({n: ("psum", list(sh), F) for n, sh in [
    ("y0", (128, 512)), ("y1", (128, 512)), ("h0", (128, 128, 4)), ("h1", (128, 128, 4)),
    ("t0", (128, 512)), ("t1", (128, 512)), ("k0", (128, 64, 8)), ("k1", (128, 64, 8))]})
NDMA = 70
SEMAPHORES = ["pe", "v", "s", "p", "sent"] + ["arr%d" % i for i in range(4)] + ["d%d" % i for i in range(NDMA)]

CY, PEC, GF, HOP, SAME = 1.04, 0.6, 1.56, 110.0, 60.0
DMAL, DMAB, REML, REMB = 1900.0, 1.0 / 180.0, 2500.0, 1.0 / 60.0
CUT = 2


def build(g, T, topo, core, rank):
    ops = []; last_w = {}; readers = {}; bank = {}; nd = [0]
    q = {"pe": g.tensor, "v": g.vector, "s": g.scalar, "p": g, "sp": g.sync}

    def op(eng, fn, rd, wr, cost, banks=(), lat=0.0, kind="c", after=(), sem=None):
        i = len(ops); deps = set()
        for k in rd:
            if k in last_w: deps.add(last_w[k])
        for k in wr:
            if k in last_w: deps.add(last_w[k])
            deps.update(readers.get(k, ()))
        for b in banks:
            st = bank.setdefault(b, {"eng": eng, "cur": [], "prev": []})
            if st["eng"] != eng:
                st["prev"] = st["cur"]; st["cur"] = []; st["eng"] = eng
            deps.update(st["prev"]); st["cur"].append(i)
        for k in rd: readers.setdefault(k, []).append(i)
        for k in wr:
            last_w[k] = i; readers[k] = []
        if kind == "dma":
            sem = "d%d" % nd[0]; nd[0] += 1
        ops.append({"eng": eng, "fn": fn, "deps": deps, "cost": cost, "lat": lat, "kind": kind, "after": set(after), "sem": sem})
        return i

    def vc(n, c=1.0): return max(64.0, n * c) * CY
    def dma(eng, out, in_, rd, wr, nbytes, after=()):
        return op(eng, lambda: q[eng].dma_start(out, in_), rd, wr, 60.0, lat=DMAL + nbytes * DMAB, kind="dma", after=after)
    def tt(out, a, b, alu, rd, wr, n, banks=(), c=1.0):
        return op("v", lambda: g.vector.tensor_tensor(out, a, b, alu), rd, wr, vc(n, c), banks)
    def ts(out, a, s1, o0, rd, wr, n, banks=(), s2=None, o1=None, c=1.0):
        if o1 is None:
            return op("v", lambda: g.vector.tensor_scalar(out, a, s1, None, o0), rd, wr, vc(n, c), banks)
        return op("v", lambda: g.vector.tensor_scalar(out, a, s1, s2, o0, o1), rd, wr, vc(n, c), banks)
    def cp(out, a, rd, wr, n, banks=(), c=1.0):
        return op("v", lambda: g.vector.tensor_copy(out, a), rd, wr, vc(n, c), banks)
    def ms(out, val, wr, n, c=1.0):
        return op("v", lambda: g.vector.memset(out, val), [], wr, vc(n, c))
    def act(out, a, rd, wr, n, banks=(), func=None, c=1.0, extra=0.0, after=(), **kw):
        f = ACT.Copy if func is None else func
        return op("s", lambda: g.scalar.activation(out, a, f, **kw), rd, wr, vc(n, c) + extra, banks, after=after)
    def mm(lst, rd, wr, cyc, banks):
        def run():
            ins = None
            for (o, l, r, st, sp) in lst: ins = g.tensor.matmul(o, l, r, st, sp)
            return ins
        return op("pe", run, rd, wr, cyc * PEC + 30.0, banks)
    def iota(out, pat, base, ch, wr, n, flt=True):
        if flt:
            return op("p", lambda: g.iota(out, pat, base, ch, allow_small_or_imprecise_dtypes=True), [], wr, 130 + 2 * n * CY)
        return op("p", lambda: g.iota(out, pat, base, ch), [], wr, 130 + 2 * n * CY)
    def asel(out, a, pat, cmp, base, ch, rd, wr, n):
        return op("p", lambda: g.affine_select(out, a, pat, cmp, 0.0, base, ch), rd, wr, 170 + 2 * n * CY)

    A, B = T.ta, T.tb
    H = [T.h0, T.h1]; Y = [T.y0, T.y1]; TR = [T.t0, T.t1]
    def hs(b, s0, s1): return H[b][:, 8 * s0:8 * s1, :]
    def half(buf, s0, s1, b): return buf[:, 8 * s0:8 * s1, 4 * b:4 * b + 4]
    def full(buf, s): return buf[:, 8 * s:8 * s + 8, :]
    def mk(i): return (T.k0 if i < 8 else T.k1)[:, 8 * (i % 8):8 * (i % 8) + 8, :]
    def both(name, *a): return [(name,) + a + (0,), (name,) + a + (1,)]
    def window(name, blocks):
        r = [(name, "i", c) for c in range(4)]
        for k in range(blocks): r += both(name, k)
        return r

    for gg in range(8):
        dma("s" if gg % 2 else "sp", T.reci[:, gg, :], T.rec[gg, :], [], [("reci", gg)], 16384)
    dma("s", T.lri[:, 0:256], T.lc[:], [], [("lri", 0)], 131072)
    dma("sp", T.lri[:, 256:512], T.rc[:], [], [("lri", 1)], 131072)
    dma("s", T.rti[:], T.rt[:], [], ["rti"], 32768)
    for c in range(2):
        dma("s" if c else "sp", T.xs[:, 2048 * c:2048 * c + 2048], T.x[:, 2048 * c:2048 * c + 2048], [], [("xs", c)], 524288, after=range(0, 11))
    dma("sp", A[:, V + 4 * K:V + 5 * K], T.nw[:], [], both("A", 4), 262144, after=range(0, 13))
    dma("s", T.wti[:, 0:1], T.wt[:], [], ["wti"], 8192)
    ms(T.ones[:], 1.0, ["ones"], 128)
    asel(T.idf[:], T.ones[:], [[-1, 128]], ALU.is_equal, 0, 1, ["ones"], ["idf"], 128)
    iota(T.pari[:, 0:4], [[-1, 4]], 4, 1, ["pari"], 4, False)
    iota(T.pari[:, 4:5], [[0, 1]], 0, 1, ["pari2"], 1, False)
    asel(T.rows[:, 16:56], T.ones[:, 0:40], [[-1, 5], [-16, 8]], ALU.is_equal, 0, 1, ["ones"], ["rows5"], 40)
    tt(T.rows[:, 0:8], T.rows[:, 16:24], T.rows[:, 24:32], ALU.add, ["rows5"], ["rowsl"], 8)
    tt(T.rows[:, 8:16], T.rows[:, 32:40], T.rows[:, 40:48], ALU.add, ["rows5", "rowsl"], ["rows"], 8)
    asel(T.tmp8[:, 0:8], T.ones[:, 0:8], [[-16, 8]], ALU.is_ge, 0, 1, ["ones"], ["tmp8"], 8)
    asel(T.sel[:], T.tmp8[:, 0:8], [[16, 8]], ALU.is_ge, 15, -1, ["tmp8"], ["sel"], 8)
    asel(T.tmp8[:], T.ones[:, 0:32], [[-4, 32]], ALU.is_ge, 0, 1, ["ones"], ["tmp8"], 32)
    asel(T.rm[:], T.tmp8[:], [[4, 32]], ALU.is_ge, 3, -1, ["tmp8"], ["rm"], 32)
    for c in range(4): ms(B[:, 1024 * c:1024 * c + 1024], 1.0, [("B", "i", c)], 1024, c=0.5)
    ms(B[:, 0:1], 0.0, [("B", "i", 0)], 1)
    ts(T.pari[:, 0:4], T.pari[:, 0:4], 3, ALU.bitwise_and, ["pari"], ["pari"], 4)
    ts(T.par[:], T.pari[:, 0:4], 0.0, ALU.is_equal, ["pari"], ["par"], 4)
    ts(T.pari[:, 4:5], T.pari[:, 4:5], 15, ALU.bitwise_and, ["pari2"], ["pari2"], 1)
    ts(T.nz[:, 0:1], T.pari[:, 4:5], 0.0, ALU.not_equal, ["pari2"], ["nz"], 1)
    cp(T.idb[:], T.idf[:], ["idf"], ["idb"], 128)
    ts(T.n8[:], T.idf[:], -8.0, ALU.mult, ["idf"], ["n8"], 128)
    ts(T.n1[:], T.idf[:], -1.0, ALU.mult, ["idf"], ["n1"], 128)
    tt(T.rme[:, 0:16], T.rows[:, 16:32], T.rows[:, 32:48], ALU.subtract, ["rows"], [("rme", 0)], 16)
    ts(T.rme[:, 16:24], T.rows[:, 0:8], -1.0, ALU.mult, ["rows"], [("rme", 1)], 8)
    cp(T.rme[:, 24:32], T.rows[:, 8:16], ["rows"], [("rme", 2)], 8)
    cp(T.rme[:, 32:48], T.rows[:, 32:48], ["rows"], [("rme", 3)], 16)
    cp(T.rme[:, 48:56], T.rows[:, 0:8], ["rows"], [("rme", 4)], 8)
    cp(T.rme[:, 56:64], T.rows[:, 48:56], ["rows"], [("rme", 5)], 8)
    cp(T.rme[:, 64:72], T.rows[:, 48:56], ["rows"], [("rme", 6)], 8)
    RME = [("rme", i) for i in range(7)]
    for e in range(4): ts(T.rmb[:, 32 * e:32 * e + 32], T.rm[:], T.par[:, e:e + 1], ALU.mult, ["rm", "par"], [("rmb", e)], 32)
    RMB = [("rmb", e) for e in range(4)]
    ms(T.zb[:], 0.0, both("zb"), 576, c=0.5)
    for i in range(4): cp(T.rg[:, 8 * i:8 * i + 8], T.sel[:], ["sel"], [("rg", i)], 8)
    RG = [("rg", i) for i in range(4)]
    cp(T.wtf[:, 0:1], T.wti[:, 0:1], ["wti"], ["wtf"], 1)
    cp(T.ws[:, 0:8], T.sel[:], ["sel"], [("ws", 0)], 8)
    ts(T.ws[:, 8:16], T.sel[:], T.wtf[:, 0:1], ALU.mult, ["sel", "wtf"], [("ws", 1)], 8)
    for j, val in enumerate([-15.5, -8.0, -14.5, -7.0, -0.5]): ms(T.bias[:, j:j + 1], val, [("bias", j)], 1)
    for t in range(3):
        for b in range(2):
            iota(T.gid[:, 80 * t:80 * t + 80, 4 * b:4 * b + 4], [[512, 10], [0, 8], [1, 4]], V + 5 * K * t - 512 + 512 * b, 4,
                 [("gid", j, b) for j in range(10 * t, 10 * t + 10)], 320)
        ms(full(T.gid, 10 * t), 1.0, both("gid", 10 * t), 64)
        if t == 0:
            iota(T.rtab[:], [[0, K]], 1, 0, ["rtab"], K)
        if t < 2:
            c0 = V + 5 * K * t + 4 * K
            iota(B[:, c0:c0 + K], [[0, K]], 1, 0, both("B", 5 * t + 4), K)
    cp(T.lrf[:], T.lri[:], [("lri", 0), ("lri", 1)], ["lrf"], 512)
    ts(T.lrf[:, 0:512:256], T.lrf[:, 0:512:256], T.nz[:, 0:1], ALU.mult, ["lrf", "nz"], ["lrf"], 2)
    BI = [("B", "i", c) for c in range(4)]
    cp(T.lr0[:], T.lrf[:], ["lrf"], ["lr0"], 512)
    tt(T.lr1[:], T.lrf[:], T.lr0[:], ALU.subtract, ["lrf", "lr0"], ["lr1"], 512, c=2)
    for j in range(4):
        dma("s" if j % 2 else "sp", B[j:128:16, 0:V], T["lr%d" % (j % 2)][:, 256 * (j // 2):256 * (j // 2) + 256], ["lr%d" % (j % 2)] + BI, [("Bi", j)], 65536)
    for e in range(2):
        cp(T.recf[:, 8 * e:8 * e + 8, :], T.reci[:, :, 16 * e:16 * e + 16], [("reci", gg) for gg in range(8)], [("recf", e)], 128)
    mm([(TR[0][:, e:256:2], T.recf[:, 8 * e:8 * e + 8, :], T.idf[:], True, True) for e in range(2)], both("recf") + ["idf"], ["t0"], 1024, ["t0"])
    cp(T.recw[:], TR[0][:, 0:256], ["t0"], ["recw"], 256, ["t0"])
    XS = [("xs", 0), ("xs", 1), "recw"]
    cp(A[:, 0:2048], T.xs[:, 0:V].indirect(T.recw[:, 0:128]), XS, [("A", "i", 0), ("A", "i", 1)], 2048, c=GF)
    act(A[:, 2048:V], T.xs[:, 0:V].indirect(T.recw[:, 128:256]), XS, [("A", "i", 2), ("A", "i", 3)], 2048, c=GF)
    ms(A[:, 0:1], 0.0, [("A", "i", 0)], 1)

    def offs(b, j): return T.off[:, 128 * b + 32 * j:128 * b + 32 * j + 32]

    def to_w(b, j, src, rd, banks, fin="off", add=0.0):
        qq = j % 2; r0 = 16 * b + 8 * qq; w = hs(b, 15 - qq, 16 - qq); hb = "h%d" % b; o = offs(b, j)
        if src is None:
            mm([(w, T.zb[:, 72 * b + 32 * p + 3 - e:72 * b + 32 * p + 35 - e, :], T.rmb[:, 32 * e:32 * e + 32], e + p == 0, e + p == 4)
                for p in range(2) for e in range(4)], [("zb", b)] + RMB, [("w", b, qq)], 512, [hb])
        else:
            for e in range(4):
                ts(T.z[:, r0:r0 + 8, 4 * e:4 * e + 4], src, T.par[:, e:e + 1], ALU.mult, rd + ["par"], [("z", b, qq, e)], 32, banks)
            mm([(w, T.z[:, r0:r0 + 8, :], T.rm[:], True, True)], [("z", b, qq, e) for e in range(4)] + ["rm"], [("w", b, qq)], 256, [hb])
        if fin == "off" and add:
            ts(o, w, add, ALU.add, [("w", b, qq)], [("off", b, j)], 32, [hb])
        elif fin == "off":
            cp(o, w, [("w", b, qq)], [("off", b, j)], 32, [hb])
        else:
            u0 = T.ui[:, 64 * b:64 * b + 32]; u1 = T.ui[:, 64 * b + 32:64 * b + 64]
            cp(u0, w, [("w", b, qq)], [("ui", b, 0)], 32, [hb])
            ts(u1, u0, K - 1, ALU.bitwise_and, [("ui", b, 0)], [("ui", b, 1)], 32)
            cp(o, u1, [("ui", b, 1)], [("off", b, j)], 32)

    def turn(bk, lhs, m, rd, out, key, split=None):
        name = "t%d" % bk
        for h in range(4):
            mm([(TR[bk][0:m, h:512:4], lhs(h), T.idf[:], True, True)], rd + ["idf"], [(name, h)] + ([name] if h == 0 else []), 512, [name])
        tk = [(name, h) for h in range(4)] + [name]
        if split:
            act(T[split + "0"][0:m, :], TR[bk][0:m, :], tk, [split + "0"], 512, [name])
            tt(T[split + "1"][0:m, :], TR[bk][0:m, :], T[split + "0"][0:m, :], ALU.subtract, tk + [split + "0"], [split + "1"], 512, [name])
        act(out[0:m, :], TR[bk][0:m, :], tk, [key], 512, [name])

    nxt_core = T.cores[(rank + 1) % len(T.cores)]
    rid, pid, _ = topo.addr(nxt_core); emask = topo.mask(core, nxt_core); neng = len(topo.engines(core, nxt_core))
    sends = {}; prev = []
    WK = {n: i for i, n in enumerate(["o2", "d", "o1", "o0", "fh0", "fh1", "fh2", "fh3", "accH", "accP", "own", "dd", "q1", "nh", "rt", "root"])}
    def wk(n): return full(T.wk, WK[n])
    def wkh(n, b): return half(T.wk, WK[n], WK[n] + 1, b)
    def lrv(f, s):
        return T.ly[:, 8 * f:8 * f + 8, 8 * s:8 * s + 8] if s < 2 else T.lx[:, 8 * f:8 * f + 8, 8 * s - 16:8 * s - 8]
    def rootv(f): return T.ly[:, 16 + 4 * f:20 + 4 * f, :]

    def last_look(t):
        Bt = V + 5 * K * t; k0 = 5 * t; ycol = Bt + 4 * K
        for b in range(2):
            hb = "h%d" % b; y = A[:, ycol + 512 * b:ycol + 512 * b + 512]; gtb = T.gt5[:, 512 * b:512 * b + 512]
            if t < 2:
                op("v", lambda gtb=gtb, y=y, b=b: g.vector.tensor_tensor(gtb, A[:, 0:Bt].indirect(offs(b, 2)), y, ALU.is_gt),
                   window("A", k0) + [("off", b, 2), ("A", k0 + 4, b)], [("gt5", b)], vc(512, GF) + 50)
            else:
                a5 = T.a5[:, 512 * b:512 * b + 512]; tn = "t%d" % b; tk = [tn] + [(tn, h) for h in range(4)]
                act(a5, A[:, 0:Bt].indirect(offs(b, 2)), window("A", k0) + [("off", b, 2)], [("a5", b)], 512, c=GF, extra=65)
                mm([(TR[b][:], T.n1[:], y, True, False)], [("A", k0 + 4, b), "n1"], tk, 512, [tn])
                mm([(TR[b][:], T.idb[:], a5, False, True)], [("a5", b), "idb"] + tk, tk, 512, [tn])
                act(gtb, TR[b][:], tk + [("bias", 4)], [("gt5", b)], 512, [tn], func=ACT.Sign, bias=T.bias[:, 4:5])
            mm([(H[b][:, 112:120, h], T.gt5[:, 512 * b + h:512 * b + 512:4], T.rg[:, 0:8], True, True) for h in range(4)], [("gt5", b)] + RG, [("w", b, 1)], 256, [hb])
            ts(half(T.hi, 16, 17, b), hs(b, 14, 15), 8.5 if t < 2 else 1.0, ALU.is_gt, [("w", b, 1)], [("hi", 4, b)], 32, [hb])
        tt(mk(15), wk("nh"), full(T.hi, 16), ALU.mult, ["nh"] + both("hi", 4), [("mk", 15)], 64, c=2)
        tt(wk("rt"), wk("nh"), lrv(0, 4), ALU.add, ["nh", ("lr", 0, 4)], ["rt"], 64, c=2)
        kr, kl = (("rv", 3), ("rv", 2)) if t < 2 else (("lr", 1, 4), ("lr", 0, 4))
        tt(rootv(3) if t < 2 else lrv(1, 4), mk(15), lrv(1, 4), ALU.add, [("mk", 15), ("lr", 1, 4)], [kr], 64)
        tt(rootv(2) if t < 2 else lrv(0, 4), wk("rt"), mk(15), ALU.subtract, [("mk", 15), "rt"], [kl], 64)

    for t in range(3):
        Bt = V + 5 * K * t; k0 = 5 * t; ycol = Bt + 4 * K
        def gs(s): return 2 * (k0 + s + 1)
        def ids(s): return 2 * (k0 + s) + 1
        for b in range(2):
            hb = "h%d" % b; yk = ("A", k0 + 4, b); y = A[:, ycol + 512 * b:ycol + 512 * b + 512]
            if t > 0:
                op("none", None, [], [yk], 0.0, kind="recv", after=[sends[(t - 1, b)]], sem="arr%d" % (2 * (t - 1) + b))
            mm([(H[b][:, 0:16, h], A[:, ycol + 512 * b + h:ycol + 512 * b + 512:4], T.ws[:], True, True) for h in range(4)],
               [yk, ("ws", 0), ("ws", 1)], [("h", b, "e")], 256, [hb])
            if t > 0:
                to_w(b, 0, hs(b, 1, 2), [("h", b, "e")], [hb], "mod")
            else:
                cp(offs(b, 0), T.rti[:, 32 * b:32 * b + 32], ["rti"], [("off", b, 0)], 32)
            cp(half(T.py, 0, 1, b), hs(b, 0, 1), [("h", b, "e")], [("py", b)], 32, [hb])
            mm([(Y[b][:], T.idb[:], y, True, True)], [yk, "idb"], [("y", b)], 512, ["y%d" % b])
        for s in range(4):
            for b in range(2):
                hb = "h%d" % b; c0 = Bt + K * s + 512 * b; ak = ("A", k0 + s, b); bk = ("B", k0 + s, b)
                lastq = s == 3 and t < 2
                if s == 0 and t > 0:
                    wa, ka, wb, kb = T.ra[:, 0:K], both("ra"), T.rtab[:, 0:K], ["rtab"] + [("rb", j) for j in range(4)]
                else:
                    wa, ka = A[:, 0:Bt + 3 * K if lastq else Bt], window("A", k0 + (3 if lastq else 0))
                    wb, kb = B[:, 0:Bt], window("B", k0) + [("Bi", j) for j in range(4)]
                ja = 1 if lastq else 0
                def ga(af): return act(A[:, c0:c0 + 512], wa.indirect(offs(b, ja)), ka + [("off", b, ja)], [ak], 512, c=GF, extra=65, after=af)
                def gb(af): return act(B[:, c0:c0 + 512], wb.indirect(offs(b, 0)), kb + [("off", b, 0)], [bk], 512, c=GF, extra=65, after=af)
                if lastq:
                    i2 = gb(prev); i1 = ga([i2])
                else:
                    i1 = ga(prev if (s or t) else []); i2 = gb([i1] if (s or t) else [])
                prev = [i1, i2]; w = 512 // CUT
                for j in range(CUT):
                    tt(T.gt[:, 512 * b + w * j:512 * b + w * j + w], A[:, c0 + w * j:c0 + w * j + w], Y[b][:, w * j:w * j + w], ALU.is_gt,
                       [ak, ("y", b)], [("gt", b, j)], w, ["y%d" % b])
                mm([(H[b][:, 104:112, h], A[:, c0 + h:c0 + 512:4], T.rg[:, 0:8], True, True) for h in range(4)], [ak] + RG, [("h", b, "p")], 256, [hb])
                mm([(H[b][:, 72:104, h], T.gt[:, 512 * b + h:512 * b + 512:4], T.rg[:], True, True) for h in range(4)],
                   [("gt", b, j) for j in range(CUT)] + RG, [("h", b, "c")], 256, [hb])
                def fe(): mm([(H[b][:, 0:72, h], B[:, c0 + h:c0 + 512:4], T.rme[:], True, True) for h in range(4)], [bk] + RME, [("h", b, "e")], 288, [hb])
                if lastq: fe()
                ts(half(T.hi, 4 * s, 4 * s + 4, b), hs(b, 9, 13), 8.5, ALU.is_gt, [("h", b, "c")], [("hi", s, b)], 128, [hb])
                if not lastq: fe()
                tt(half(T.pr, 4 * s, 4 * s + 4, b), hs(b, 0, 4), half(T.hi, 4 * s, 4 * s + 4, b), ALU.mult, [("h", b, "e"), ("hi", s, b)], [("pr", s, b)], 128, [hb])
                tt(T.zb[:, 72 * b + 3:72 * b + 67:4, :], hs(b, 4, 6), half(T.pr, 4 * s, 4 * s + 2, b), ALU.add, [("h", b, "e"), ("pr", s, b)], [("zb", b)], 64, [hb])
                nx = half(T.nk, 2 * s, 2 * s + 1, b)
                if s == 3 or (s == 2 and t < 2):
                    tt(nx, T.zb[:, 72 * b + 3:72 * b + 35:4, :], T.zb[:, 72 * b + 35:72 * b + 67:4, :], ALU.add, [("zb", b)], [("nx", b)], 32, c=2)
                def gp():
                    tt(half(T.nk, 2 * s + 1, 2 * s + 2, b), hs(b, 6, 7), half(T.pr, 4 * s + 2, 4 * s + 3, b), ALU.add, [("h", b, "e"), ("pr", s, b)], [("nk", s, b)], 32, [hb])
                    tt(half(T.glp, 2 * s, 2 * s + 2, b), hs(b, 7, 9), half(T.gid, 2 * (k0 + s), 2 * (k0 + s) + 2, b), ALU.mult,
                       [("h", b, "e"), ("gid", 2 * (k0 + s), b), ("gid", ids(s), b)], [("glp", s, b)], 64, [hb])
                    tt(T.k1[:, 32:40, 4 * b:4 * b + 4], hs(b, 13, 14), half(T.py, 0, 1, b), ALU.is_lt, [("h", b, "p"), ("py", b)], [("mk", 12, b)], 32, [hb])
                if s == 2 and t < 2:
                    to_w(b, 0, None, [], [])
                    gp()
                    ow = wkh("own", b); dd = wkh("dd", b); q1 = wkh("q1", b)
                    tt(ow, ow, half(T.glp, 5, 6, b), ALU.max, [("own", b), ("glp", 2, b)], [("own", b)], 32, c=2)
                    ts(dd, nx, 0.0, ALU.is_equal, [("nx", b)], [("dd", b)], 32, s2=65536.0, o1=ALU.mult)
                    tt(dd, dd, ow, ALU.min, [("dd", b), ("own", b)], [("dd", b)], 32, c=2)
                    tt(q1, dd, nx, ALU.add, [("dd", b), ("nx", b)], [("q1", b)], 32, c=2)
                    to_w(b, 1, q1, [("q1", b)], [])
                elif s == 3:
                    gp()
                    to_w(b, 2, None, [], [])
                else:
                    to_w(b, 0, None, [], [])
                    gp()
                    if s == 1 and t < 2:
                        to_w(b, 3, wkh("root", b), ["root"], [], add=-float(Bt))
                if lastq:
                    tn = "t%d" % b; yn = "y%d" % b; y = A[:, ycol + 512 * b:ycol + 512 * b + 512]; yk = ("A", k0 + 4, b)
                    tk = [tn] + [(tn, h) for h in range(4)]
                    sgn = T.sg[:, 512 * b:512 * b + 512]; so = T.sb[:, K * t + 512 * b:K * t + 512 * b + 512]
                    mm([(TR[b][:], T.idb[:], y, True, False)], [yk, "idb"], tk, 512, [tn])
                    mm([(TR[b][:], T.idb[:], A[:, c0:c0 + 512], False, True)], [ak, "idb"] + tk, tk, 512, [tn])
                    act(sgn, TR[b][:], tk + [("bias", 2 * t)], [("sg", b)], 512, [tn], func=ACT.Sign, bias=T.bias[:, 2 * t:2 * t + 1])
                    mm([(Y[b][:], T.idb[:], y, True, False), (Y[b][:], T.idb[:], A[:, c0:c0 + 512], False, False)], ["idb", yk, ak], [("y", b)], 1024, [yn])
                    mm([(Y[b][:], T.n8[:], sgn, False, True)], ["n8", ("sg", b), ("y", b)], [("y", b)], 512, [yn])
                    act(so, Y[b][:], [("y", b), ("bias", 2 * t + 1)], [("sb", t, b)], 512, [yn], func=ACT.Identity, bias=T.bias[:, 2 * t + 1:2 * t + 2])
                    dst = A[:, ycol + 5 * K + 512 * b:ycol + 5 * K + 512 * b + 512]
                    def send(dst=dst, so=so, nm="arr%d" % (2 * t + b)):
                        return g.remote_dma(dst, so, T.sem[nm], T.sem.sent, pid, rid, emask)
                    sends[(t, b)] = op("p", send, [("sb", t, b)], [], 300.0, lat=REML + 131072 * REMB, kind="send")
            if s == 0 and t > 0:
                last_look(t - 1)
            gl = full(T.glp, 2 * s); P = full(T.glp, 2 * s + 1); hi = full(T.hi, 4 * s); M = full(T.gid, ids(4)); MK = both("gid", ids(4))
            tt(mk(13), mk(12), gl, ALU.mult, both("mk", 12) + both("glp", s), [("mk", 13)], 64)
            tt(full(T.gid, gs(s)), gl, mk(13), ALU.subtract, both("glp", s) + [("mk", 13)], both("gid", gs(s)), 64)
            if s == 0:
                tt(wk("accH"), mk(13), hi, ALU.mult, [("mk", 13)] + both("hi", s), ["accH"], 64)
                tt(wk("accP"), mk(13), P, ALU.mult, [("mk", 13)] + both("glp", s), ["accP"], 64)
                ts(mk(14), full(T.gid, gs(0)), -4096.0, ALU.mult, both("gid", gs(0)), [("mk", 14)], 64)
                tt(wk("root") if t < 2 else rootv(0), mk(14), M, ALU.add, [("mk", 14)] + MK, ["root" if t < 2 else ("rv", 0)], 64)
            else:
                tt(mk(14), mk(13), hi, ALU.mult, [("mk", 13)] + both("hi", s), [("mk", 14)], 64)
                tt(mk(15), mk(13), P, ALU.mult, [("mk", 13)] + both("glp", s), [("mk", 15)], 64)
                tt(wk("accH"), mk(14), wk("accH"), ALU.add, [("mk", 14), "accH"], ["accH"], 64)
                tt(wk("accP"), mk(15), wk("accP"), ALU.add, [("mk", 15), "accP"], ["accP"], 64)
                r = s - 1
                tt(mk(8 + r), full(T.hi, 4 * r), hi, ALU.is_equal, both("hi", r) + both("hi", s), [("mk", 8 + r)], 64, c=2)
                tt(mk(8 + r), mk(8 + r), full(T.gid, gs(r)), ALU.max, [("mk", 8 + r)] + both("gid", gs(r)), [("mk", 8 + r)], 64)
                tt(mk(r), full(T.gid, gs(r)), full(T.gid, gs(s)), ALU.subtract, both("gid", gs(r)) + both("gid", gs(s)), [("mk", r)], 64, c=2)
                tt(mk(r), mk(r), M, ALU.mult, [("mk", r)] + MK, [("mk", r)], 64)
            if s == 1 and t < 2:
                tt(wk("own"), full(T.glp, 1), P, ALU.max, both("glp", 0) + both("glp", 1), both("own"), 64, c=2)
        if t < 2:
            for b in range(2):
                act(T.ra[:, 512 * b:512 * b + 512], A[:, Bt:Bt + 5 * K].indirect(offs(b, 3)),
                    [k for j in range(5) for k in both("A", k0 + j)] + [("off", b, 3)], [("ra", b)], 512, c=GF, extra=65, after=[sends[(t, 1)]])
        g3 = full(T.gid, gs(3)); G3 = both("gid", gs(3)); nx3 = full(T.nk, 6)
        tt(mk(3), g3, M, ALU.mult, G3 + MK, [("mk", 3)], 64, c=2)
        tt(wk("nh"), g3, nx3, ALU.mult, G3 + both("nx"), ["nh"], 64, c=2)
        tt(wk("fh3"), nx3, wk("nh"), ALU.subtract, both("nx") + ["nh"], ["fh3"], 64, c=2)
        tt(wk("fh2"), mk(10), full(T.glp, 7), ALU.mult, [("mk", 10)] + both("glp", 3), ["fh2"], 64)
        tt(wk("o2"), full(T.glp, 7), wk("fh2"), ALU.subtract, both("glp", 3) + ["fh2"], ["o2"], 64, c=2)
        for s in (1, 0):
            P = full(T.glp, 2 * s + 3); PK = both("glp", s + 1); on = "o%d" % (s + 1)
            tt(wk("d"), P, wk(on), ALU.subtract, PK + [on], ["d"], 64, c=2)
            tt(mk(11), mk(8 + s), wk("d"), ALU.mult, [("mk", 8 + s), "d"], [("mk", 11)], 64)
            tt(wk("o%d" % s), P, mk(11), ALU.subtract, PK + [("mk", 11)], ["o%d" % s], 64)
            tt(wk("fh%d" % s), mk(11), wk(on), ALU.add, [("mk", 11), on], ["fh%d" % s], 64)
        for s in (3, 2, 1, 0):
            tt(mk(s), mk(s), wk("fh%d" % s), ALU.max, [("mk", s), "fh%d" % s], [("mk", s)], 64)
            tt(mk(4 + s), mk(s), full(T.hi, 4 * s), ALU.mult, [("mk", s)] + both("hi", s), [("mk", 4 + s)], 64)
            tt(wk("fh%d" % s), mk(s), full(T.pr, 4 * s + 3), ALU.add, [("mk", s)] + both("pr", s), ["fh%d" % s], 64)
            tt(lrv(0, s), mk(4 + s), full(T.nk, 2 * s + 1), ALU.add, [("mk", 4 + s)] + both("nk", s), [("lr", 0, s)], 64)
            tt(lrv(1, s), wk("fh%d" % s), mk(4 + s), ALU.subtract, [("mk", 4 + s), "fh%d" % s], [("lr", 1, s)], 64)
        tt(mk(14), wk("accP"), wk("o0"), ALU.subtract, ["accP", "o0"], [("mk", 14)], 64, c=2)
        tt(mk(14), mk(14), wk("accH"), ALU.mult, [("mk", 14), "accH"], [("mk", 14)], 64)
        tt(lrv(0, 4), wk("accP"), mk(14), ALU.subtract, ["accP", ("mk", 14)], [("lr", 0, 4)], 64)
        tt(lrv(1, 4), mk(14), wk("o0"), ALU.add, ["o0", ("mk", 14)], [("lr", 1, 4)], 64)
        if t < 2:
            for f in range(2):
                tt(mk(8 + f), lrv(f, 0), lrv(f, 4), ALU.subtract, [("lr", f, 0), ("lr", f, 4)], [("mk", 8 + f)], 64, c=2)
                tt(mk(8 + f), mk(8 + f), full(T.gid, gs(0)), ALU.mult, [("mk", 8 + f)] + both("gid", gs(0)), [("mk", 8 + f)], 64)
                tt(rootv(f), mk(8 + f), lrv(f, 4), ALU.add, [("mk", 8 + f), ("lr", f, 4)], [("rv", f)], 64)
        else:
            last_look(t)
        my = 128 if t else 96
        turn(0, lambda h: T.ly[:, 0:my // 4, h:16:4], my, [("lr", f, s) for f in range(2) for s in range(2)] + [("rv", j) for j in range(4)],
             T.oy, "oy", "sy" if t < 2 else None)
        turn(1, lambda h: T.lx[:, :, h:24:4], 96, [("lr", f, s) for f in range(2) for s in (2, 3, 4)], T.ox, "ox", "sx" if t < 2 else None)
        if t < 2:
            for j in range(4):
                f, p = j // 2, "%d" % (j % 2)
                dma("sp", T.rtab[j:128:16, :], T["sy" + p][64 + 16 * f:80 + 16 * f, :], ["sy" + p, "rtab"], [("rb", j)], 16384)
            for j in range(4):
                f, p = j // 2, "%d" % (j % 2)
                dma("sp", B[j:128:16, Bt:Bt + 2 * K], T["sy" + p][32 * f:32 * f + 32, :], ["sy" + p], [("Bu", j, 0)], 32768)
                dma("sp", B[j:128:16, Bt + 2 * K:Bt + 5 * K], T["sx" + p][48 * f:48 * f + 48, :], ["sx" + p] + both("B", k0 + 4), [("Bu", j, 1)], 49152)
                if t == 1:
                    dma("sp", B[j:128:16, V + 4 * K:V + 5 * K], T["sy" + p][96 + 16 * f:112 + 16 * f, :], ["sy" + p], [("Bu", j, 2)], 16384)
            op("none", None, [("Bu", f, j) for f in range(4) for j in range(3)], both("B", k0 + 4), 0.0, kind="join")
        else:
            dma("s", T.yt[:], T.oy[64:80, :], ["oy"], [], 32768)
        for f in range(2):
            yo = T.yr if f else T.yl
            dma("sp", yo[:, 5 * K * t:5 * K * t + 2 * K], T.oy[32 * f:32 * f + 32, :], ["oy"], [], 65536)
            dma("s" if t == 2 and f else "sp", yo[:, 5 * K * t + 2 * K:5 * K * t + 5 * K], T.ox[48 * f:48 * f + 48, :], ["ox"], [("yo", t, f)], 98304)
            if t:
                dma("sp", yo[:, 5 * K * t - K:5 * K * t], T.oy[96 + 16 * f:112 + 16 * f, :], ["oy"], [("yo", t - 1, f)], 32768)
    return ops, q, neng


def schedule(ops):
    n = len(ops); succ = [[] for _ in range(n)]
    for i, o in enumerate(ops):
        for d in o["deps"] | o["after"]: succ[d].append(i)
    rank = [0.0] * n
    for i in range(n - 1, -1, -1):
        rank[i] = ops[i]["cost"] + ops[i]["lat"] + max([rank[j] + HOP for j in succ[i]], default=0.0)
    left = [len(o["deps"] | o["after"]) for o in ops]; ready = [0.0] * n; fin = [0.0] * n; start = [0.0] * n
    free = {"pe": 0.0, "v": 0.0, "s": 0.0, "p": 0.0, "sp": 0.0}; order = {e: [] for e in free}
    pool = [i for i in range(n) if left[i] == 0]; dmafree = [0.0]

    def done(i):
        for j in succ[i]:
            hop = 0.0 if ops[i]["eng"] == "none" else (SAME if ops[i]["eng"] == ops[j]["eng"] and ops[i]["kind"] == "c" else HOP)
            hard = i in ops[j]["deps"] or ops[j]["kind"] == "recv"
            ready[j] = max(ready[j], fin[i] + hop if hard else start[i] + ops[i]["cost"]); left[j] -= 1
            if left[j] == 0: pool.append(j)
    while pool:
        z = [i for i in pool if ops[i]["eng"] == "none"]
        if z:
            for i in z:
                pool.remove(i); start[i] = fin[i] = ready[i]; done(i)
            continue
        t0, e = min((max(ready[i], free[ops[i]["eng"]]), ops[i]["eng"]) for i in pool)
        cand = [i for i in pool if ops[i]["eng"] == e]
        now = [i for i in cand if ready[i] <= t0 + 1e-9]
        i = max(now, key=lambda j: (rank[j], -j))
        soon = [j for j in cand if t0 < ready[j] < t0 + 0.5 * ops[i]["cost"] and rank[j] > rank[i] + 2 * ops[i]["cost"]]
        if soon: i = max(soon, key=lambda j: (rank[j], -j))
        pool.remove(i); start[i] = max(ready[i], free[e]); free[e] = start[i] + ops[i]["cost"]
        if ops[i]["kind"] == "dma":
            dmafree[0] = max(dmafree[0], free[e]) + ops[i]["lat"] - DMAL; fin[i] = dmafree[0] + DMAL
        else:
            fin[i] = free[e] + ops[i]["lat"]
        order[e].append(i); done(i)
    return order, start, fin


def rank_program(g, core, T, topo):
    rank = T.rank_of(core)
    if rank is None:
        return
    ops, q, neng = build(g, T, topo, core, rank)
    order, start, fin = schedule(ops)
    mark = {}; count = {"pe": 0, "v": 0, "s": 0, "p": 0}; total = {}
    for e in order:
        for i in order[e]:
            if ops[i]["kind"] == "c":
                count[e] += 1; mark[i] = [(e, count[e])]
            elif ops[i]["kind"] == "dma":
                mark[i] = [(ops[i]["sem"], 16)]; total[ops[i]["sem"]] = 16
    for i, o in enumerate(ops):
        if o["kind"] == "recv":
            mark[i] = [(o["sem"], neng)] + [w for d in o["deps"] for w in mark[d]]; total[o["sem"]] = neng
        elif o["kind"] == "join":
            mark[i] = [w for d in o["deps"] for w in mark[d]]
    for e in order:
        seen = {}
        for i in order[e]:
            need = {}
            for d in ops[i]["deps"]:
                for (s, v) in mark[d]:
                    if e == "pe" and s == "pe": continue
                    need[s] = max(need.get(s, 0), v)
            for s in sorted(need):
                if need[s] > seen.get(s, 0):
                    q[e].wait_ge(T.sem[s], need[s]); seen[s] = need[s]
            ins = ops[i]["fn"]()
            if ops[i]["kind"] == "c": ins.then_inc(T.sem[e], 1)
            elif ops[i]["kind"] == "dma": ins.then_inc(T.sem[ops[i]["sem"]], 16)
    total.update(count); total["sent"] = 4 * neng
    for s in sorted(total):
        g.wait_ge(T.sem[s], total[s])
